import numpy as np
import ml_dtypes


def mxq(x, axis, fmt="e4m3"):
    dtype, down = {"e4m3": (ml_dtypes.float8_e4m3fn, 7), "e5m2": (ml_dtypes.float8_e5m2, 14)}[fmt]
    v = np.moveaxis(np.asarray(x, np.float32).astype(ml_dtypes.bfloat16).astype(np.float64), axis, -1)
    blocks = v.reshape(v.shape[:-1] + (-1, 32))
    amax = np.abs(blocks).max(-1, keepdims=True)
    byte = np.maximum(np.where(amax > 0, np.frexp(amax)[1] - 1 + 127, 0) - down, 1)
    scale = np.exp2(byte - 127.0)
    codes = (blocks / scale).astype(np.float32).astype(dtype).astype(np.float64)
    return np.moveaxis((codes * scale).reshape(v.shape), -1, axis)


WIDE = False


def mx_kscale(k):
    if not WIDE:
        return np.ones(k)
    levels = np.array([10, -10, 5, -5, 0])
    if k % 512:
        return np.exp2(np.random.permutation(np.resize(levels, k // 32))).repeat(32)
    a = np.empty((k // 512, 16))
    for p in range(k // 512):
        a[p, :8] = np.random.permutation(np.resize(levels, 8))
        for g in range(8):
            far = levels[np.abs(levels - a[p, g]) >= 10]
            a[p, g + 8] = far[np.random.randint(len(far))]
    return np.exp2(a.ravel()).repeat(32)


def f64(x):
    return np.asarray(x).astype(np.float64)


def striped(idx):
    return np.tile(idx.reshape(-1, 16).T, (8, 1)).astype(np.uint16)


def unstriped(offs):
    return offs[:16].T.reshape(-1).astype(np.int64)


def striped8(idx):
    return np.concatenate([x.reshape(-1, 16).T for x in idx]).astype(np.uint16)


def runs(offs, k):
    lists = np.stack([offs[16 * r : 16 * r + 16].T.reshape(-1) for r in range(8)]).astype(np.int64)
    return lists[np.arange(k) % 512 // 64]


def pack_weight(w):
    k, n = w.shape
    w = f64(np.asarray(w, np.float32).astype(ml_dtypes.bfloat16)).reshape(k // 32, 32, n)
    amax = np.abs(w).max(1)
    byte = np.clip(np.where(amax > 0, np.frexp(amax)[1] - 1 + 127 - 7, 1), 1, 254)
    scaled = (w * np.exp2(127.0 - byte)[:, None, :]).reshape(k, n).astype(np.float32)
    words = np.ascontiguousarray(scaled.reshape(k // 512, 128, 4, n).transpose(0, 1, 3, 2)).astype(ml_dtypes.float8_e4m3fn).view(np.uint8)
    return words, np.ascontiguousarray(byte.astype(np.uint8).reshape(k // 512, 16, n))


def unpack_weight(words, scales):
    g, p, n, _ = words.shape
    vals = np.ascontiguousarray(words).view(ml_dtypes.float8_e4m3fn).astype(np.float64) * np.repeat(np.exp2(scales.astype(np.float64) - 127.0), 8, axis=1)[..., None]
    return vals.transpose(0, 1, 3, 2).reshape(g * 512, n)


K, T, S, N, H, U = 512, 2048, 512, 512, 512, 512


def setup_inputs():
    n = np.random.standard_normal
    s = mx_kscale(K)[:, None]
    u = mx_kscale(H)
    packed_xT = pack_weight(n((K, T)) * s)
    return {
        "x_words": packed_xT[0],
        "x_scales": packed_xT[1],
        "w1": (n((K, H)) / np.sqrt(K) / s * u).astype(np.float32),
        "w2": (n((K, H)) / np.sqrt(K) / s).astype(np.float32),
        "noise": np.random.uniform(0.1, 0.6, (H, U)).astype(np.float32),
        "w3": (n((H, N)) / np.sqrt(H) / u[:, None]).astype(np.float32),
        "offs": striped(np.random.permutation(T)[:S]),
        "pr": striped8(np.random.randint(0, U, (8, S))),
    }


def reference(x_words, x_scales, w1, w2, noise, w3, offs, pr):
    xq = unpack_weight(x_words, x_scales)[:, unstriped(offs)]
    re = mxq(f64(w1), 0, "e4m3").T @ xq
    im = mxq(f64(w2), 0, "e4m3").T @ xq
    mg = np.sqrt((im) ** 2 + 0.25)
    ga = np.maximum(mg - (f64(noise)[np.arange(H)[:, None], runs(pr, H)]), 0.25 * mg)
    z = re * (ga / mg)
    return mxq(f64(w3), 0, "e4m3").T @ mxq(z, 0, "e4m3")

@@ -1,0 +1,212 @@
+from contextlib import ExitStack
+
+import concourse.mybir as mybir
+
+K, T, S, H, U, N = 512, 2048, 512, 512, 512, 512
+FLOPS = 2 * K * H * S * 2 + 2 * H * N * S
+
+F32 = mybir.dt.float32
+BF16 = mybir.dt.bfloat16
+I32 = mybir.dt.int32
+U32 = mybir.dt.uint32
+U16 = mybir.dt.uint16
+U8 = mybir.dt.uint8
+FP8X4 = mybir.dt.float8_e4m3fn_x4
+ACT = mybir.ActivationFunctionType
+ALU = mybir.AluOpType
+
+P = 128
+PACK = 4
+CHUNK = 128
+CHUNKS = S // CHUNK
+HALF = 256
+
+
+def tile_picked_specsub_none_p_kernel(
+    tc, x_words, x_scales, w1, w2, noise, w3, offs, pr, out
+):
+    nc = tc.nc
+    with ExitStack() as ctx:
+        keep = ctx.enter_context(tc.tile_pool(name="keep", bufs=1))
+        psum = ctx.enter_context(tc.psum_pool(name="psum", bufs=4))
+
+        pr_sb = keep.tile([P, S // 16], U16, name="pr_sb")
+        nc.sync.dma_start(pr_sb[:], pr)
+        noise_rows = noise.rearrange("(p t) u -> p t u", t=PACK)
+        noise_sb = [keep.tile([P, U], F32, name=f"noise{t}") for t in range(PACK)]
+        for t in (0, 1):
+            nc.sync.dma_start(noise_sb[t][:], noise_rows[:, t, :])
+        offs_sb = keep.tile([P, S // 16], U16, name="offs_sb")
+        nc.sync.dma_start(offs_sb[:], offs)
+        xw_all = keep.tile([P, T], I32, name="xw_all")
+        nc.sync.dma_start(xw_all[:], x_words[0].rearrange("p n t -> p (n t)").bitcast(I32))
+
+        def load_halves(w, name):
+            rows = w.rearrange("(p j) c -> p j c", j=PACK)
+            halves = [keep.tile([P, PACK, HALF], F32, name=f"{name}_raw{h}") for h in range(2)]
+            for h in range(2):
+                nc.sync.dma_start(halves[h][:], rows[:, :, h * HALF : (h + 1) * HALF])
+            return halves
+
+        w2_raw = load_halves(w2, "w2")
+        for t in (2, 3):
+            nc.sync.dma_start(noise_sb[t][:], noise_rows[:, t, :])
+        w1_raw = load_halves(w1, "w1")
+        w3_raw = keep.tile([P, PACK, N], F32, name="w3_raw")
+        nc.sync.dma_start(w3_raw[:], w3.rearrange("(p j) c -> p j c", j=PACK))
+
+        xs_all = keep.tile([P, T], U8, name="xs_all")
+        nc.vector.memset(xs_all[:].bitcast(I32), 0)
+        for q in range(4):
+            nc.scalar.dma_start(
+                xs_all[32 * q : 32 * q + 4, :].bitcast(I32), x_scales[0, 4 * q : 4 * q + 4, :].bitcast(I32)
+            )
+
+        warm_in = keep.tile([P, 8], F32, name="warm_in")
+        warm_out = keep.tile([P, 8], F32, name="warm_out")
+        nc.gpsimd.memset(warm_in[:], 1.0)
+        nc.scalar.activation(warm_out[:], warm_in[:], ACT.Abs_reciprocal_sqrt, bias=0.25)
+
+        picked = [keep.tile([P, PACK, HALF], F32, name=f"picked{h}") for h in range(2)]
+
+        def gather_noise(t):
+            for h in range(2):
+                nc.vector.tensor_copy(picked[h][:, t, :], noise_sb[t][:].indirect(pr_sb[:, 16 * h : 16 * h + 16]))
+
+        gather_noise(0)
+        gather_noise(1)
+        xs = keep.tile([P, S], U8, name="xs", align_bytes=64)
+        nc.vector.tensor_copy(xs[:], xs_all[:].indirect(offs_sb[:]))
+        xw = keep.tile([P, S], U32, name="xw", align_bytes=64)
+        nc.vector.tensor_copy(xw[:], xw_all[:].bitcast(U32).indirect(offs_sb[:]))
+
+        def quantize(grouped, width, name):
+            codes = keep.tile([P, width], U32, name=f"{name}_codes", align_bytes=64)
+            scales = keep.tile([P, width], U8, name=f"{name}_scales", align_bytes=64)
+            nc.vector.quantize_mx(out=codes[:].bitcast(FP8X4), scales=scales[:], in_=grouped)
+            return codes, scales
+
+        def regroup(copy, grouped, halves, m0, m1):
+            h, lo = divmod(m0, 64)
+            copy(
+                grouped[:].rearrange("p t m j -> p m j t")[:, m0:m1],
+                halves[h][:].rearrange("p j (m t) -> p m j t", t=PACK)[:, lo : lo + m1 - m0],
+            )
+
+        def project(bank, codes, scales, rhs, rhs_scales, first=0, count=PACK):
+            for t in range(count):
+                cols = slice((first + t) * P, (first + t + 1) * P)
+                nc.tensor.matmul_mx(
+                    out=bank[:, t, :],
+                    lhsT=codes[:, cols].bitcast(FP8X4),
+                    lhsT_scale=scales[:, cols],
+                    rhs=rhs.bitcast(FP8X4),
+                    rhs_scale=rhs_scales,
+                    start=True,
+                    stop=True,
+                )
+
+        w2_grouped = keep.tile([P, PACK, P, PACK], BF16, name="w2_grouped", align_bytes=64)
+        regroup(nc.scalar.copy, w2_grouped, w2_raw, 0, 64)
+        regroup(nc.scalar.copy, w2_grouped, w2_raw, 64, 88)
+        regroup(nc.vector.tensor_copy, w2_grouped, w2_raw, 88, 128)
+        w2_codes, w2_scales = quantize(w2_grouped[:].rearrange("p t m j -> p (t m j)"), H, "w2")
+        gather_noise(2)
+        gather_noise(3)
+
+        w1_grouped = keep.tile([P, PACK, P, PACK], BF16, name="w1_grouped", align_bytes=64)
+        inv_mag = []
+        for c in range(CHUNKS):
+            cols = slice(c * CHUNK, (c + 1) * CHUNK)
+            im = psum.tile([P, PACK, CHUNK], F32, name="im", tag="outer")
+            project(im, w2_codes, w2_scales, xw[:, cols], xs[:, cols])
+            sq = keep.tile([P, PACK, CHUNK], F32, name=f"sq{c}")
+            nc.scalar.activation(sq[:], im[:], ACT.Square)
+            r = keep.tile([P, PACK, CHUNK], F32, name=f"inv_mag{c}")
+            nc.scalar.activation(r[:], sq[:], ACT.Abs_reciprocal_sqrt, bias=0.25)
+            inv_mag.append(r)
+            if c == 0:
+                regroup(nc.scalar.copy, w1_grouped, w1_raw, 0, 64)
+
+        regroup(nc.vector.tensor_copy, w1_grouped, w1_raw, 64, 128)
+        w1_codes, w1_scales = quantize(w1_grouped[:].rearrange("p t m j -> p (t m j)"), H, "w1")
+        re = []
+        for c in range(CHUNKS):
+            cols = slice(c * CHUNK, (c + 1) * CHUNK)
+            bank = psum.tile([P, PACK, CHUNK], F32, name="re", tag="re")
+            project(bank, w1_codes, w1_scales, xw[:, cols], xs[:, cols])
+            re.append(bank)
+
+        w3_grouped = keep.tile([P, N, PACK], BF16, name="w3_grouped", align_bytes=64)
+        for mt in range(PACK):
+            cols = slice(mt * P, (mt + 1) * P)
+            nc.scalar.copy(
+                w3_grouped[:, cols, :].rearrange("p (c i) j -> p c j i", i=4),
+                w3_raw[:, :, cols].rearrange("p j (c i) -> p c j i", i=4),
+            )
+
+        ratio, gain, z, zq = {}, {}, {}, {}
+
+        def step_ratio(c):
+            ratio[c] = keep.tile([P, PACK, CHUNK], F32, name=f"ratio{c}")
+            h, lo = divmod(c * CHUNK, HALF)
+            nc.vector.scalar_tensor_tensor(
+                ratio[c][:], picked[h][:, :, lo : lo + CHUNK], -1.0, inv_mag[c][:], ALU.mult, ALU.mult
+            )
+
+        def step_gain(c):
+            gain[c] = keep.tile([P, PACK, CHUNK], F32, name=f"gain{c}")
+            nc.vector.tensor_scalar(gain[c][:], ratio[c][:], 1.0, 0.25, ALU.add, ALU.max)
+
+        def step_z(c):
+            z[c] = keep.tile([P, CHUNK, PACK], BF16, name=f"z{c}", align_bytes=64)
+            nc.vector.tensor_tensor(
+                z[c][:].rearrange("p (c i) t -> p c t i", i=4),
+                gain[c][:].rearrange("p t (c i) -> p c t i", i=4),
+                re[c][:].rearrange("p t (c i) -> p c t i", i=4),
+                ALU.mult,
+            )
+
+        def step_quantize(c):
+            zq[c] = quantize(z[c][:].rearrange("p n t -> p (n t)"), CHUNK, f"z{c}")
+
+        out_rows = out.rearrange("(mt p) j -> p mt j", p=P)
+
+        def step_out(c, w3q):
+            cols = slice(c * CHUNK, (c + 1) * CHUNK)
+            bank = psum.tile([P, PACK, CHUNK], F32, name="acc", tag="outer")
+            project(bank, w3q[0], w3q[1], zq[c][0][:], zq[c][1][:])
+            res = keep.tile([P, PACK, CHUNK], F32, name=f"res{c}")
+            nc.scalar.copy(res[:], bank[:])
+            nc.sync.dma_start(out_rows[:, :, cols], res[:])
+
+        def step_out_last(c, w3q):
+            cols = slice(c * CHUNK, (c + 1) * CHUNK)
+            for u, (copy, queue) in enumerate(((nc.scalar.copy, nc.scalar), (nc.vector.tensor_copy, nc.sync))):
+                bank = psum.tile([P, 2, CHUNK], F32, name="acc", tag="re")
+                project(bank, w3q[0], w3q[1], zq[c][0][:], zq[c][1][:], 2 * u, 2)
+                res = keep.tile([P, 2, CHUNK], F32, name=f"last{u}")
+                copy(res[:], bank[:])
+                queue.dma_start(out_rows[:, 2 * u : 2 * u + 2, cols], res[:])
+
+        step_ratio(0)
+        step_ratio(1)
+        step_gain(0)
+        step_gain(1)
+        step_z(0)
+        step_ratio(2)
+        step_quantize(0)
+        step_z(1)
+        step_gain(2)
+        step_quantize(1)
+        step_ratio(3)
+        step_z(2)
+        step_gain(3)
+        w3q = quantize(w3_grouped[:].rearrange("p n j -> p (n j)"), N, "w3")
+        step_out(0, w3q)
+        step_out(1, w3q)
+        step_z(3)
+        step_quantize(2)
+        step_out(2, w3q)
+        step_quantize(3)
+        step_out_last(3, w3q)

@@ -30,37 +30,36 @@ def tile_picked_specsub_none_p_kernel(
         keep = ctx.enter_context(tc.tile_pool(name="keep", bufs=1))
         psum = ctx.enter_context(tc.psum_pool(name="psum", bufs=4))
 
+        xs_all = keep.tile([P, T], U8, name="xs_all")
+        nc.vector.memset(xs_all[:].bitcast(I32), 0)
         pr_sb = keep.tile([P, S // 16], U16, name="pr_sb")
         nc.sync.dma_start(pr_sb[:], pr)
         noise_rows = noise.rearrange("(p t) u -> p t u", t=PACK)
         noise_sb = [keep.tile([P, U], F32, name=f"noise{t}") for t in range(PACK)]
-        for t in (0, 1):
-            nc.sync.dma_start(noise_sb[t][:], noise_rows[:, t, :])
+        nc.sync.dma_start(noise_sb[0][:], noise_rows[:, 0, :])
         offs_sb = keep.tile([P, S // 16], U16, name="offs_sb")
         nc.sync.dma_start(offs_sb[:], offs)
+        for r in range(4):
+            nc.sync.dma_start(xs_all[r:P:32, :].bitcast(I32), x_scales[0, r:16:4, :].bitcast(I32))
         xw_all = keep.tile([P, T], I32, name="xw_all")
         nc.sync.dma_start(xw_all[:], x_words[0].rearrange("p n t -> p (n t)").bitcast(I32))
+        nc.sync.dma_start(noise_sb[1][:], noise_rows[:, 1, :])
 
-        def load_halves(w, name):
+        def load_half(w, name, h):
+            raw = keep.tile([P, PACK, HALF], F32, name=f"{name}_raw{h}")
             rows = w.rearrange("(p j) c -> p j c", j=PACK)
-            halves = [keep.tile([P, PACK, HALF], F32, name=f"{name}_raw{h}") for h in range(2)]
-            for h in range(2):
-                nc.sync.dma_start(halves[h][:], rows[:, :, h * HALF : (h + 1) * HALF])
-            return halves
+            nc.sync.dma_start(raw[:], rows[:, :, h * HALF : (h + 1) * HALF])
+            return raw
 
-        w2_raw = load_halves(w2, "w2")
-        for t in (2, 3):
-            nc.sync.dma_start(noise_sb[t][:], noise_rows[:, t, :])
-        w1_raw = load_halves(w1, "w1")
+        w2_raw, w1_raw = [], []
+        w2_raw.append(load_half(w2, "w2", 0))
+        nc.sync.dma_start(noise_sb[2][:], noise_rows[:, 2, :])
+        w2_raw.append(load_half(w2, "w2", 1))
+        w1_raw.append(load_half(w1, "w1", 0))
+        nc.sync.dma_start(noise_sb[3][:], noise_rows[:, 3, :])
+        w1_raw.append(load_half(w1, "w1", 1))
         w3_raw = keep.tile([P, PACK, N], F32, name="w3_raw")
         nc.sync.dma_start(w3_raw[:], w3.rearrange("(p j) c -> p j c", j=PACK))
-
-        xs_all = keep.tile([P, T], U8, name="xs_all")
-        nc.vector.memset(xs_all[:].bitcast(I32), 0)
-        for q in range(4):
-            nc.scalar.dma_start(
-                xs_all[32 * q : 32 * q + 4, :].bitcast(I32), x_scales[0, 4 * q : 4 * q + 4, :].bitcast(I32)
-            )
 
         warm_in = keep.tile([P, 8], F32, name="warm_in")
         warm_out = keep.tile([P, 8], F32, name="warm_out")
@@ -74,11 +73,11 @@ def tile_picked_specsub_none_p_kernel(
                 nc.vector.tensor_copy(picked[h][:, t, :], noise_sb[t][:].indirect(pr_sb[:, 16 * h : 16 * h + 16]))
 
         gather_noise(0)
-        gather_noise(1)
         xs = keep.tile([P, S], U8, name="xs", align_bytes=64)
         nc.vector.tensor_copy(xs[:], xs_all[:].indirect(offs_sb[:]))
         xw = keep.tile([P, S], U32, name="xw", align_bytes=64)
         nc.vector.tensor_copy(xw[:], xw_all[:].bitcast(U32).indirect(offs_sb[:]))
+        gather_noise(1)
 
         def quantize(grouped, width, name):
             codes = keep.tile([P, width], U32, name=f"{name}_codes", align_bytes=64)
@@ -86,11 +85,10 @@ def tile_picked_specsub_none_p_kernel(
             nc.vector.quantize_mx(out=codes[:].bitcast(FP8X4), scales=scales[:], in_=grouped)
             return codes, scales
 
-        def regroup(copy, grouped, halves, m0, m1):
-            h, lo = divmod(m0, 64)
+        def regroup(copy, grouped, halves, h, u):
             copy(
-                grouped[:].rearrange("p t m j -> p m j t")[:, m0:m1],
-                halves[h][:].rearrange("p j (m t) -> p m j t", t=PACK)[:, lo : lo + m1 - m0],
+                grouped[:].rearrange("p t m j -> p m j t")[:, 64 * h : 64 * h + 64, :, 2 * u : 2 * u + 2],
+                halves[h][:].rearrange("p j (m t) -> p m j t", t=PACK)[:, :, :, 2 * u : 2 * u + 2],
             )
 
         def project(bank, codes, scales, rhs, rhs_scales, first=0, count=PACK):
@@ -107,14 +105,17 @@ def tile_picked_specsub_none_p_kernel(
                 )
 
         w2_grouped = keep.tile([P, PACK, P, PACK], BF16, name="w2_grouped", align_bytes=64)
-        regroup(nc.scalar.copy, w2_grouped, w2_raw, 0, 64)
-        regroup(nc.scalar.copy, w2_grouped, w2_raw, 64, 88)
-        regroup(nc.vector.tensor_copy, w2_grouped, w2_raw, 88, 128)
-        w2_codes, w2_scales = quantize(w2_grouped[:].rearrange("p t m j -> p (t m j)"), H, "w2")
+        regroup(nc.scalar.copy, w2_grouped, w2_raw, 0, 0)
+        regroup(nc.scalar.copy, w2_grouped, w2_raw, 0, 1)
         gather_noise(2)
+        regroup(nc.scalar.copy, w2_grouped, w2_raw, 1, 1)
+        regroup(nc.vector.tensor_copy, w2_grouped, w2_raw, 1, 0)
+        w2_codes, w2_scales = quantize(w2_grouped[:].rearrange("p t m j -> p (t m j)"), H, "w2")
         gather_noise(3)
 
         w1_grouped = keep.tile([P, PACK, P, PACK], BF16, name="w1_grouped", align_bytes=64)
+        regroup(nc.scalar.copy, w1_grouped, w1_raw, 0, 0)
+        regroup(nc.scalar.copy, w1_grouped, w1_raw, 0, 1)
         inv_mag = []
         for c in range(CHUNKS):
             cols = slice(c * CHUNK, (c + 1) * CHUNK)
@@ -125,10 +126,9 @@ def tile_picked_specsub_none_p_kernel(
             r = keep.tile([P, PACK, CHUNK], F32, name=f"inv_mag{c}")
             nc.scalar.activation(r[:], sq[:], ACT.Abs_reciprocal_sqrt, bias=0.25)
             inv_mag.append(r)
-            if c == 0:
-                regroup(nc.scalar.copy, w1_grouped, w1_raw, 0, 64)
 
-        regroup(nc.vector.tensor_copy, w1_grouped, w1_raw, 64, 128)
+        regroup(nc.vector.tensor_copy, w1_grouped, w1_raw, 1, 0)
+        regroup(nc.vector.tensor_copy, w1_grouped, w1_raw, 1, 1)
         w1_codes, w1_scales = quantize(w1_grouped[:].rearrange("p t m j -> p (t m j)"), H, "w1")
         re = []
         for c in range(CHUNKS):
@@ -141,8 +141,8 @@ def tile_picked_specsub_none_p_kernel(
         for mt in range(PACK):
             cols = slice(mt * P, (mt + 1) * P)
             nc.scalar.copy(
-                w3_grouped[:, cols, :].rearrange("p (c i) j -> p c j i", i=4),
-                w3_raw[:, :, cols].rearrange("p j (c i) -> p c j i", i=4),
+                w3_grouped[:, cols, :].rearrange("p (c i) j -> p c j i", i=2),
+                w3_raw[:, :, cols].rearrange("p j (c i) -> p c j i", i=2),
             )
 
         ratio, gain, z, zq = {}, {}, {}, {}
@@ -161,9 +161,9 @@ def tile_picked_specsub_none_p_kernel(
         def step_z(c):
             z[c] = keep.tile([P, CHUNK, PACK], BF16, name=f"z{c}", align_bytes=64)
             nc.vector.tensor_tensor(
-                z[c][:].rearrange("p (c i) t -> p c t i", i=4),
-                gain[c][:].rearrange("p t (c i) -> p c t i", i=4),
-                re[c][:].rearrange("p t (c i) -> p c t i", i=4),
+                z[c][:].rearrange("p (c i) t -> p c t i", i=2),
+                gain[c][:].rearrange("p t (c i) -> p c t i", i=2),
+                re[c][:].rearrange("p t (c i) -> p c t i", i=2),
                 ALU.mult,
             )
 

@@ -39,11 +39,11 @@ def tile_picked_specsub_none_p_kernel(
         nc.sync.dma_start(noise_sb[0][:], noise_rows[:, 0, :])
         offs_sb = keep.tile([P, S // 16], U16, name="offs_sb")
         nc.sync.dma_start(offs_sb[:], offs)
-        for r in range(4):
-            nc.sync.dma_start(xs_all[r:P:32, :].bitcast(I32), x_scales[0, r:16:4, :].bitcast(I32))
+        nc.sync.dma_start(noise_sb[1][:], noise_rows[:, 1, :])
         xw_all = keep.tile([P, T], I32, name="xw_all")
         nc.sync.dma_start(xw_all[:], x_words[0].rearrange("p n t -> p (n t)").bitcast(I32))
-        nc.sync.dma_start(noise_sb[1][:], noise_rows[:, 1, :])
+        for r in range(4):
+            nc.sync.dma_start(xs_all[r:P:32, :].bitcast(I32), x_scales[0, r:16:4, :].bitcast(I32))
 
         def load_half(w, name, h):
             raw = keep.tile([P, PACK, HALF], F32, name=f"{name}_raw{h}")
@@ -53,12 +53,12 @@ def tile_picked_specsub_none_p_kernel(
 
         w2_raw, w1_raw = [], []
         w2_raw.append(load_half(w2, "w2", 0))
-        nc.sync.dma_start(noise_sb[2][:], noise_rows[:, 2, :])
         w2_raw.append(load_half(w2, "w2", 1))
         w1_raw.append(load_half(w1, "w1", 0))
+        nc.sync.dma_start(noise_sb[2][:], noise_rows[:, 2, :])
         nc.sync.dma_start(noise_sb[3][:], noise_rows[:, 3, :])
         w1_raw.append(load_half(w1, "w1", 1))
-        w3_raw = keep.tile([P, PACK, N], F32, name="w3_raw")
+        w3_raw = keep.tile([P, PACK, N], F32, name="w3_raw", tag="w3_then_sq")
         nc.sync.dma_start(w3_raw[:], w3.rearrange("(p j) c -> p j c", j=PACK))
 
         warm_in = keep.tile([P, 8], F32, name="warm_in")
@@ -73,11 +73,11 @@ def tile_picked_specsub_none_p_kernel(
                 nc.vector.tensor_copy(picked[h][:, t, :], noise_sb[t][:].indirect(pr_sb[:, 16 * h : 16 * h + 16]))
 
         gather_noise(0)
-        xs = keep.tile([P, S], U8, name="xs", align_bytes=64)
-        nc.vector.tensor_copy(xs[:], xs_all[:].indirect(offs_sb[:]))
+        gather_noise(1)
         xw = keep.tile([P, S], U32, name="xw", align_bytes=64)
         nc.vector.tensor_copy(xw[:], xw_all[:].bitcast(U32).indirect(offs_sb[:]))
-        gather_noise(1)
+        xs = keep.tile([P, S], U8, name="xs", align_bytes=64)
+        nc.vector.tensor_copy(xs[:], xs_all[:].indirect(offs_sb[:]))
 
         def quantize(grouped, width, name):
             codes = keep.tile([P, width], U32, name=f"{name}_codes", align_bytes=64)
@@ -107,21 +107,32 @@ def tile_picked_specsub_none_p_kernel(
         w2_grouped = keep.tile([P, PACK, P, PACK], BF16, name="w2_grouped", align_bytes=64)
         regroup(nc.scalar.copy, w2_grouped, w2_raw, 0, 0)
         regroup(nc.scalar.copy, w2_grouped, w2_raw, 0, 1)
-        gather_noise(2)
         regroup(nc.scalar.copy, w2_grouped, w2_raw, 1, 1)
         regroup(nc.vector.tensor_copy, w2_grouped, w2_raw, 1, 0)
         w2_codes, w2_scales = quantize(w2_grouped[:].rearrange("p t m j -> p (t m j)"), H, "w2")
+        gather_noise(2)
         gather_noise(3)
 
         w1_grouped = keep.tile([P, PACK, P, PACK], BF16, name="w1_grouped", align_bytes=64)
         regroup(nc.scalar.copy, w1_grouped, w1_raw, 0, 0)
         regroup(nc.scalar.copy, w1_grouped, w1_raw, 0, 1)
+        w3_grouped = keep.tile([P, N, PACK], BF16, name="w3_grouped", align_bytes=64)
+
+        def regroup3(copy, lo, hi):
+            copy(
+                w3_grouped[:, lo:hi, :].rearrange("p (c i) j -> p c j i", i=2),
+                w3_raw[:, :, lo:hi].rearrange("p j (c i) -> p c j i", i=2),
+            )
+
         inv_mag = []
         for c in range(CHUNKS):
+            if c == CHUNKS - 1:
+                regroup3(nc.vector.tensor_copy, 384, 512)
+                regroup3(nc.scalar.copy, 0, 384)
             cols = slice(c * CHUNK, (c + 1) * CHUNK)
             im = psum.tile([P, PACK, CHUNK], F32, name="im", tag="outer")
             project(im, w2_codes, w2_scales, xw[:, cols], xs[:, cols])
-            sq = keep.tile([P, PACK, CHUNK], F32, name=f"sq{c}")
+            sq = keep.tile([P, PACK, CHUNK], F32, name=f"sq{c}", tag="w3_then_sq" if c == CHUNKS - 1 else f"sq{c}")
             nc.scalar.activation(sq[:], im[:], ACT.Square)
             r = keep.tile([P, PACK, CHUNK], F32, name=f"inv_mag{c}")
             nc.scalar.activation(r[:], sq[:], ACT.Abs_reciprocal_sqrt, bias=0.25)
@@ -136,14 +147,6 @@ def tile_picked_specsub_none_p_kernel(
             bank = psum.tile([P, PACK, CHUNK], F32, name="re", tag="re")
             project(bank, w1_codes, w1_scales, xw[:, cols], xs[:, cols])
             re.append(bank)
-
-        w3_grouped = keep.tile([P, N, PACK], BF16, name="w3_grouped", align_bytes=64)
-        for mt in range(PACK):
-            cols = slice(mt * P, (mt + 1) * P)
-            nc.scalar.copy(
-                w3_grouped[:, cols, :].rearrange("p (c i) j -> p c j i", i=2),
-                w3_raw[:, :, cols].rearrange("p j (c i) -> p c j i", i=2),
-            )
 
         ratio, gain, z, zq = {}, {}, {}, {}
 
@@ -199,14 +202,14 @@ def tile_picked_specsub_none_p_kernel(
         step_z(1)
         step_gain(2)
         step_quantize(1)
-        step_ratio(3)
-        step_z(2)
-        step_gain(3)
         w3q = quantize(w3_grouped[:].rearrange("p n j -> p (n j)"), N, "w3")
         step_out(0, w3q)
         step_out(1, w3q)
-        step_z(3)
+        step_ratio(3)
+        step_z(2)
+        step_gain(3)
         step_quantize(2)
         step_out(2, w3q)
+        step_z(3)
         step_quantize(3)
         step_out_last(3, w3q)

@@ -20,6 +20,8 @@ PACK = 4
 CHUNK = 128
 CHUNKS = S // CHUNK
 HALF = 256
+PAIR = 2
+LIST_ROWS = 16
 
 
 def tile_picked_specsub_none_p_kernel(
@@ -28,49 +30,53 @@ def tile_picked_specsub_none_p_kernel(
     nc = tc.nc
     with ExitStack() as ctx:
         keep = ctx.enter_context(tc.tile_pool(name="keep", bufs=1))
-        psum = ctx.enter_context(tc.psum_pool(name="psum", bufs=4))
+        psum = ctx.enter_context(tc.psum_pool(name="psum", bufs=CHUNKS))
 
         xs_all = keep.tile([P, T], U8, name="xs_all")
         nc.vector.memset(xs_all[:].bitcast(I32), 0)
-        pr_sb = keep.tile([P, S // 16], U16, name="pr_sb")
-        nc.sync.dma_start(pr_sb[:], pr)
+
         noise_rows = noise.rearrange("(p t) u -> p t u", t=PACK)
         noise_sb = [keep.tile([P, U], F32, name=f"noise{t}") for t in range(PACK)]
-        nc.sync.dma_start(noise_sb[0][:], noise_rows[:, 0, :])
-        offs_sb = keep.tile([P, S // 16], U16, name="offs_sb")
+
+        def load_noise(t):
+            nc.sync.dma_start(noise_sb[t][:], noise_rows[:, t, :])
+
+        def load_weight(w, cols, name):
+            raw = keep.tile([P, PACK, cols.stop - cols.start], F32, name=name, tag=name)
+            nc.sync.dma_start(raw[:], w.rearrange("(p j) c -> p j c", j=PACK)[:, :, cols])
+            return raw
+
+        pr_sb = keep.tile([P, S // LIST_ROWS], U16, name="pr_sb")
+        nc.sync.dma_start(pr_sb[:], pr)
+        load_noise(0)
+        offs_sb = keep.tile([P, S // LIST_ROWS], U16, name="offs_sb")
         nc.sync.dma_start(offs_sb[:], offs)
-        nc.sync.dma_start(noise_sb[1][:], noise_rows[:, 1, :])
+        load_noise(1)
         xw_all = keep.tile([P, T], I32, name="xw_all")
         nc.sync.dma_start(xw_all[:], x_words[0].rearrange("p n t -> p (n t)").bitcast(I32))
         for r in range(4):
             nc.sync.dma_start(xs_all[r:P:32, :].bitcast(I32), x_scales[0, r:16:4, :].bitcast(I32))
+        w2_raw = load_weight(w2, slice(0, H), "w2_raw")
+        w1_raw = []
+        for h in range(2):
+            load_noise(2 + h)
+            w1_raw.append(load_weight(w1, slice(h * HALF, (h + 1) * HALF), f"w1_raw{h}"))
+        w3_raw = load_weight(w3, slice(0, N), "w3_raw")
 
-        def load_half(w, name, h):
-            raw = keep.tile([P, PACK, HALF], F32, name=f"{name}_raw{h}")
-            rows = w.rearrange("(p j) c -> p j c", j=PACK)
-            nc.sync.dma_start(raw[:], rows[:, :, h * HALF : (h + 1) * HALF])
-            return raw
+        sixteen = keep.tile([P, 1], F32, name="sixteen")
+        quarter = keep.tile([P, 1], F32, name="quarter")
+        nc.gpsimd.memset(sixteen[:], 16.0)
+        nc.scalar.activation(quarter[:], sixteen[:], ACT.Abs_reciprocal_sqrt)
 
-        w2_raw, w1_raw = [], []
-        w2_raw.append(load_half(w2, "w2", 0))
-        w2_raw.append(load_half(w2, "w2", 1))
-        w1_raw.append(load_half(w1, "w1", 0))
-        nc.sync.dma_start(noise_sb[2][:], noise_rows[:, 2, :])
-        nc.sync.dma_start(noise_sb[3][:], noise_rows[:, 3, :])
-        w1_raw.append(load_half(w1, "w1", 1))
-        w3_raw = keep.tile([P, PACK, N], F32, name="w3_raw", tag="w3_then_sq")
-        nc.sync.dma_start(w3_raw[:], w3.rearrange("(p j) c -> p j c", j=PACK))
-
-        warm_in = keep.tile([P, 8], F32, name="warm_in")
-        warm_out = keep.tile([P, 8], F32, name="warm_out")
-        nc.gpsimd.memset(warm_in[:], 1.0)
-        nc.scalar.activation(warm_out[:], warm_in[:], ACT.Abs_reciprocal_sqrt, bias=0.25)
-
-        picked = [keep.tile([P, PACK, HALF], F32, name=f"picked{h}") for h in range(2)]
+        staging_at = 2 * S + HALF
+        shared = keep.tile([P, staging_at + H * PACK // 2], F32, name="shared", align_bytes=64)
+        picked = shared[:, : PACK * S].rearrange("p (t n) -> p t n", t=PACK)
+        w2_staged = shared[:, staging_at:].bitcast(BF16)
 
         def gather_noise(t):
             for h in range(2):
-                nc.vector.tensor_copy(picked[h][:, t, :], noise_sb[t][:].indirect(pr_sb[:, 16 * h : 16 * h + 16]))
+                entries = pr_sb[:, h * HALF // LIST_ROWS : (h + 1) * HALF // LIST_ROWS]
+                nc.vector.tensor_copy(picked[:, t, h * HALF : (h + 1) * HALF], noise_sb[t][:].indirect(entries))
 
         gather_noise(0)
         gather_noise(1)
@@ -79,137 +85,123 @@ def tile_picked_specsub_none_p_kernel(
         xs = keep.tile([P, S], U8, name="xs", align_bytes=64)
         nc.vector.tensor_copy(xs[:], xs_all[:].indirect(offs_sb[:]))
 
-        def quantize(grouped, width, name):
+        def quantize(staged, name):
+            width = staged.shape[1] // PACK
             codes = keep.tile([P, width], U32, name=f"{name}_codes", align_bytes=64)
             scales = keep.tile([P, width], U8, name=f"{name}_scales", align_bytes=64)
-            nc.vector.quantize_mx(out=codes[:].bitcast(FP8X4), scales=scales[:], in_=grouped)
+            nc.vector.quantize_mx(out=codes[:].bitcast(FP8X4), scales=scales[:], in_=staged)
             return codes, scales
 
-        def regroup(copy, grouped, halves, h, u):
+        def stage_dealt(copy, staged, raw, u, first):
+            count = raw.shape[2] // PACK
+            planes = slice(PAIR * u, PAIR * (u + 1))
             copy(
-                grouped[:].rearrange("p t m j -> p m j t")[:, 64 * h : 64 * h + 64, :, 2 * u : 2 * u + 2],
-                halves[h][:].rearrange("p j (m t) -> p m j t", t=PACK)[:, :, :, 2 * u : 2 * u + 2],
+                staged.rearrange("p (t m j) -> p m j t", t=PACK, j=PACK)[:, first : first + count, :, planes],
+                raw.rearrange("p j (m t) -> p m j t", t=PACK)[:, :, :, planes],
             )
 
-        def project(bank, codes, scales, rhs, rhs_scales, first=0, count=PACK):
-            for t in range(count):
-                cols = slice((first + t) * P, (first + t + 1) * P)
+        def multiply(bank, weight, first, moving, cols):
+            for a in range(bank.shape[1]):
+                rows = slice((first + a) * P, (first + a + 1) * P)
                 nc.tensor.matmul_mx(
-                    out=bank[:, t, :],
-                    lhsT=codes[:, cols].bitcast(FP8X4),
-                    lhsT_scale=scales[:, cols],
-                    rhs=rhs.bitcast(FP8X4),
-                    rhs_scale=rhs_scales,
+                    out=bank[:, a, :],
+                    lhsT=weight[0][:, rows].bitcast(FP8X4),
+                    lhsT_scale=weight[1][:, rows],
+                    rhs=moving[0][:, cols].bitcast(FP8X4),
+                    rhs_scale=moving[1][:, cols],
                     start=True,
                     stop=True,
                 )
 
-        w2_grouped = keep.tile([P, PACK, P, PACK], BF16, name="w2_grouped", align_bytes=64)
-        regroup(nc.scalar.copy, w2_grouped, w2_raw, 0, 0)
-        regroup(nc.scalar.copy, w2_grouped, w2_raw, 0, 1)
-        regroup(nc.scalar.copy, w2_grouped, w2_raw, 1, 1)
-        regroup(nc.vector.tensor_copy, w2_grouped, w2_raw, 1, 0)
-        w2_codes, w2_scales = quantize(w2_grouped[:].rearrange("p t m j -> p (t m j)"), H, "w2")
+        def chunk(c):
+            return slice(c * CHUNK, (c + 1) * CHUNK)
+
+        stage_dealt(nc.scalar.copy, w2_staged, w2_raw[:], 1, 0)
+        stage_dealt(nc.vector.tensor_copy, w2_staged, w2_raw[:], 0, 0)
+        w2_mx = quantize(w2_staged, "w2")
         gather_noise(2)
         gather_noise(3)
 
-        w1_grouped = keep.tile([P, PACK, P, PACK], BF16, name="w1_grouped", align_bytes=64)
-        regroup(nc.scalar.copy, w1_grouped, w1_raw, 0, 0)
-        regroup(nc.scalar.copy, w1_grouped, w1_raw, 0, 1)
-        w3_grouped = keep.tile([P, N, PACK], BF16, name="w3_grouped", align_bytes=64)
+        w1_staged = keep.tile([P, H * PACK], BF16, name="w1_staged", align_bytes=64)
+        for u in range(2):
+            stage_dealt(nc.scalar.copy, w1_staged[:], w1_raw[0][:], u, 0)
 
-        def regroup3(copy, lo, hi):
-            copy(
-                w3_grouped[:, lo:hi, :].rearrange("p (c i) j -> p c j i", i=2),
-                w3_raw[:, :, lo:hi].rearrange("p j (c i) -> p c j i", i=2),
-            )
-
+        w3_staged = keep.tile([P, N, PACK], BF16, name="w3_staged", align_bytes=64)
         inv_mag = []
         for c in range(CHUNKS):
-            if c == CHUNKS - 1:
-                regroup3(nc.vector.tensor_copy, 384, 512)
-                regroup3(nc.scalar.copy, 0, 384)
-            cols = slice(c * CHUNK, (c + 1) * CHUNK)
-            im = psum.tile([P, PACK, CHUNK], F32, name="im", tag="outer")
-            project(im, w2_codes, w2_scales, xw[:, cols], xs[:, cols])
-            sq = keep.tile([P, PACK, CHUNK], F32, name=f"sq{c}", tag="w3_then_sq" if c == CHUNKS - 1 else f"sq{c}")
-            nc.scalar.activation(sq[:], im[:], ACT.Square)
-            r = keep.tile([P, PACK, CHUNK], F32, name=f"inv_mag{c}")
-            nc.scalar.activation(r[:], sq[:], ACT.Abs_reciprocal_sqrt, bias=0.25)
-            inv_mag.append(r)
+            im = psum.tile([P, PACK, CHUNK], F32, name="im", tag="im")
+            multiply(im, w2_mx, 0, (xw, xs), chunk(c))
+            square = keep.tile([P, PACK, CHUNK], F32, name=f"square{c}")
+            nc.scalar.activation(square[:], im[:], ACT.Square)
+            last = c == CHUNKS - 1
+            if last:
+                nc.scalar.copy(
+                    w3_staged[:].rearrange("p (c i) j -> p c j i", i=PAIR),
+                    w3_raw[:].rearrange("p j (c i) -> p c j i", i=PAIR),
+                )
+            inv = keep.tile([P, PACK, CHUNK], F32, name=f"inv_mag{c}", tag="w3_raw" if last else f"inv_mag{c}")
+            nc.scalar.activation(inv[:], square[:], ACT.Abs_reciprocal_sqrt, bias=quarter[:])
+            inv_mag.append(inv)
 
-        regroup(nc.vector.tensor_copy, w1_grouped, w1_raw, 1, 0)
-        regroup(nc.vector.tensor_copy, w1_grouped, w1_raw, 1, 1)
-        w1_codes, w1_scales = quantize(w1_grouped[:].rearrange("p t m j -> p (t m j)"), H, "w1")
+        for u in range(2):
+            stage_dealt(nc.vector.tensor_copy, w1_staged[:], w1_raw[1][:], u, P // 2)
+        w1_mx = quantize(w1_staged[:], "w1")
         re = []
         for c in range(CHUNKS):
-            cols = slice(c * CHUNK, (c + 1) * CHUNK)
             bank = psum.tile([P, PACK, CHUNK], F32, name="re", tag="re")
-            project(bank, w1_codes, w1_scales, xw[:, cols], xs[:, cols])
+            multiply(bank, w1_mx, 0, (xw, xs), chunk(c))
             re.append(bank)
 
-        ratio, gain, z, zq = {}, {}, {}, {}
+        z_first = keep.tile([P, 2 * CHUNK, PACK], BF16, name="z_first", align_bytes=64)
+        z_third = keep.tile([P, CHUNK, PACK], BF16, name="z_third", align_bytes=64)
+        z_last = keep.tile([P, CHUNK, PACK], BF16, name="z_last", align_bytes=64)
+        z = [z_first[:, chunk(0), :], z_first[:, chunk(1), :], z_third[:], z_last[:]]
+        ratio = [keep.tile([P, PACK, CHUNK], F32, name=f"ratio{c}") for c in range(CHUNKS)]
+        gain = [keep.tile([P, PACK, CHUNK], F32, name=f"gain{c}") for c in range(CHUNKS)]
+        out_rows = out.rearrange("(a p) j -> p a j", p=P)
 
-        def step_ratio(c):
-            ratio[c] = keep.tile([P, PACK, CHUNK], F32, name=f"ratio{c}")
-            h, lo = divmod(c * CHUNK, HALF)
-            nc.vector.scalar_tensor_tensor(
-                ratio[c][:], picked[h][:, :, lo : lo + CHUNK], -1.0, inv_mag[c][:], ALU.mult, ALU.mult
-            )
+        def make_ratio(c):
+            nc.vector.scalar_tensor_tensor(ratio[c][:], picked[:, :, chunk(c)], -1.0, inv_mag[c][:], ALU.mult, ALU.mult)
 
-        def step_gain(c):
-            gain[c] = keep.tile([P, PACK, CHUNK], F32, name=f"gain{c}")
+        def make_gain(c):
             nc.vector.tensor_scalar(gain[c][:], ratio[c][:], 1.0, 0.25, ALU.add, ALU.max)
 
-        def step_z(c):
-            z[c] = keep.tile([P, CHUNK, PACK], BF16, name=f"z{c}", align_bytes=64)
+        def make_z(c):
             nc.vector.tensor_tensor(
-                z[c][:].rearrange("p (c i) t -> p c t i", i=2),
-                gain[c][:].rearrange("p t (c i) -> p c t i", i=2),
-                re[c][:].rearrange("p t (c i) -> p c t i", i=2),
+                z[c].rearrange("p (c i) t -> p c t i", i=PAIR),
+                gain[c][:].rearrange("p t (c i) -> p c t i", i=PAIR),
+                re[c][:].rearrange("p t (c i) -> p c t i", i=PAIR),
                 ALU.mult,
             )
 
-        def step_quantize(c):
-            zq[c] = quantize(z[c][:].rearrange("p n t -> p (n t)"), CHUNK, f"z{c}")
+        def quantize_z(tile, name):
+            return quantize(tile[:].rearrange("p n t -> p (n t)"), name)
 
-        out_rows = out.rearrange("(mt p) j -> p mt j", p=P)
+        def emit(z_mx, frame0, first, count, tag, copy, queue):
+            width = z_mx[0].shape[1]
+            bank = psum.tile([P, count, width], F32, name="acc", tag=tag)
+            multiply(bank, w3_mx, first, z_mx, slice(0, width))
+            result = keep.tile([P, count, width], F32, name=f"result{frame0}_{first}")
+            copy(result[:], bank[:])
+            queue.dma_start(out_rows[:, first : first + count, frame0 : frame0 + width], result[:])
 
-        def step_out(c, w3q):
-            cols = slice(c * CHUNK, (c + 1) * CHUNK)
-            bank = psum.tile([P, PACK, CHUNK], F32, name="acc", tag="outer")
-            project(bank, w3q[0], w3q[1], zq[c][0][:], zq[c][1][:])
-            res = keep.tile([P, PACK, CHUNK], F32, name=f"res{c}")
-            nc.scalar.copy(res[:], bank[:])
-            nc.sync.dma_start(out_rows[:, :, cols], res[:])
-
-        def step_out_last(c, w3q):
-            cols = slice(c * CHUNK, (c + 1) * CHUNK)
-            for u, (copy, queue) in enumerate(((nc.scalar.copy, nc.scalar), (nc.vector.tensor_copy, nc.sync))):
-                bank = psum.tile([P, 2, CHUNK], F32, name="acc", tag="re")
-                project(bank, w3q[0], w3q[1], zq[c][0][:], zq[c][1][:], 2 * u, 2)
-                res = keep.tile([P, 2, CHUNK], F32, name=f"last{u}")
-                copy(res[:], bank[:])
-                queue.dma_start(out_rows[:, 2 * u : 2 * u + 2, cols], res[:])
-
-        step_ratio(0)
-        step_ratio(1)
-        step_gain(0)
-        step_gain(1)
-        step_z(0)
-        step_ratio(2)
-        step_quantize(0)
-        step_z(1)
-        step_gain(2)
-        step_quantize(1)
-        w3q = quantize(w3_grouped[:].rearrange("p n j -> p (n j)"), N, "w3")
-        step_out(0, w3q)
-        step_out(1, w3q)
-        step_ratio(3)
-        step_z(2)
-        step_gain(3)
-        step_quantize(2)
-        step_out(2, w3q)
-        step_z(3)
-        step_quantize(3)
-        step_out_last(3, w3q)
+        make_ratio(0)
+        make_ratio(1)
+        make_gain(0)
+        make_gain(1)
+        make_z(0)
+        make_z(1)
+        make_ratio(2)
+        z_first_mx = quantize_z(z_first, "z_first")
+        make_gain(2)
+        w3_mx = quantize(w3_staged[:].rearrange("p n j -> p (n j)"), "w3")
+        for first in (0, 2):
+            emit(z_first_mx, 0, first, 2, "im", nc.scalar.copy, nc.sync)
+        make_ratio(3)
+        make_z(2)
+        make_gain(3)
+        emit(quantize_z(z_third, "z_third"), 2 * CHUNK, 0, PACK, "im", nc.scalar.copy, nc.sync)
+        make_z(3)
+        z_last_mx = quantize_z(z_last, "z_last")
+        emit(z_last_mx, 3 * CHUNK, 0, 2, "re", nc.scalar.copy, nc.scalar)
+        emit(z_last_mx, 3 * CHUNK, 2, 2, "re", nc.vector.tensor_copy, nc.sync)

from contextlib import ExitStack

import concourse.mybir as mybir

K, T, S, H, U, N = 512, 2048, 512, 512, 512, 512
FLOPS = 2 * K * H * S * 2 + 2 * H * N * S

F32 = mybir.dt.float32
BF16 = mybir.dt.bfloat16
I32 = mybir.dt.int32
U32 = mybir.dt.uint32
U16 = mybir.dt.uint16
U8 = mybir.dt.uint8
FP8X4 = mybir.dt.float8_e4m3fn_x4
ACT = mybir.ActivationFunctionType
ALU = mybir.AluOpType

P = 128
PACK = 4
CHUNK = 128
CHUNKS = S // CHUNK
HALF = 256
PAIR = 2
LIST_ROWS = 16


def tile_picked_specsub_none_p_kernel(
    tc, x_words, x_scales, w1, w2, noise, w3, offs, pr, out
):
    nc = tc.nc
    with ExitStack() as ctx:
        keep = ctx.enter_context(tc.tile_pool(name="keep", bufs=1))
        psum = ctx.enter_context(tc.psum_pool(name="psum", bufs=CHUNKS))

        xs_all = keep.tile([P, T], U8, name="xs_all")
        nc.vector.memset(xs_all[:].bitcast(I32), 0)

        noise_rows = noise.rearrange("(p t) u -> p t u", t=PACK)
        noise_sb = [keep.tile([P, U], F32, name=f"noise{t}") for t in range(PACK)]

        def load_noise(t):
            nc.sync.dma_start(noise_sb[t][:], noise_rows[:, t, :])

        def load_weight(w, cols, name):
            raw = keep.tile([P, PACK, cols.stop - cols.start], F32, name=name, tag=name)
            nc.sync.dma_start(raw[:], w.rearrange("(p j) c -> p j c", j=PACK)[:, :, cols])
            return raw

        pr_sb = keep.tile([P, S // LIST_ROWS], U16, name="pr_sb")
        nc.sync.dma_start(pr_sb[:], pr)
        load_noise(0)
        offs_sb = keep.tile([P, S // LIST_ROWS], U16, name="offs_sb")
        nc.sync.dma_start(offs_sb[:], offs)
        load_noise(1)
        xw_all = keep.tile([P, T], I32, name="xw_all")
        nc.sync.dma_start(xw_all[:], x_words[0].rearrange("p n t -> p (n t)").bitcast(I32))
        for r in range(4):
            nc.sync.dma_start(xs_all[r:P:32, :].bitcast(I32), x_scales[0, r:16:4, :].bitcast(I32))
        w2_raw = load_weight(w2, slice(0, H), "w2_raw")
        w1_raw = []
        for h in range(2):
            load_noise(2 + h)
            w1_raw.append(load_weight(w1, slice(h * HALF, (h + 1) * HALF), f"w1_raw{h}"))
        w3_raw = load_weight(w3, slice(0, N), "w3_raw")

        sixteen = keep.tile([P, 1], F32, name="sixteen")
        quarter = keep.tile([P, 1], F32, name="quarter")
        nc.gpsimd.memset(sixteen[:], 16.0)
        nc.scalar.activation(quarter[:], sixteen[:], ACT.Abs_reciprocal_sqrt)

        staging_at = 2 * S + HALF
        shared = keep.tile([P, staging_at + H * PACK // 2], F32, name="shared", align_bytes=64)
        picked = shared[:, : PACK * S].rearrange("p (t n) -> p t n", t=PACK)
        w2_staged = shared[:, staging_at:].bitcast(BF16)

        def gather_noise(t):
            for h in range(2):
                entries = pr_sb[:, h * HALF // LIST_ROWS : (h + 1) * HALF // LIST_ROWS]
                nc.vector.tensor_copy(picked[:, t, h * HALF : (h + 1) * HALF], noise_sb[t][:].indirect(entries))

        gather_noise(0)
        gather_noise(1)
        xw = keep.tile([P, S], U32, name="xw", align_bytes=64)
        nc.vector.tensor_copy(xw[:], xw_all[:].bitcast(U32).indirect(offs_sb[:]))
        xs = keep.tile([P, S], U8, name="xs", align_bytes=64)
        nc.vector.tensor_copy(xs[:], xs_all[:].indirect(offs_sb[:]))

        def quantize(staged, name):
            width = staged.shape[1] // PACK
            codes = keep.tile([P, width], U32, name=f"{name}_codes", align_bytes=64)
            scales = keep.tile([P, width], U8, name=f"{name}_scales", align_bytes=64)
            nc.vector.quantize_mx(out=codes[:].bitcast(FP8X4), scales=scales[:], in_=staged)
            return codes, scales

        def stage_dealt(copy, staged, raw, u, first):
            count = raw.shape[2] // PACK
            planes = slice(PAIR * u, PAIR * (u + 1))
            copy(
                staged.rearrange("p (t m j) -> p m j t", t=PACK, j=PACK)[:, first : first + count, :, planes],
                raw.rearrange("p j (m t) -> p m j t", t=PACK)[:, :, :, planes],
            )

        def multiply(bank, weight, first, moving, cols):
            for a in range(bank.shape[1]):
                rows = slice((first + a) * P, (first + a + 1) * P)
                nc.tensor.matmul_mx(
                    out=bank[:, a, :],
                    lhsT=weight[0][:, rows].bitcast(FP8X4),
                    lhsT_scale=weight[1][:, rows],
                    rhs=moving[0][:, cols].bitcast(FP8X4),
                    rhs_scale=moving[1][:, cols],
                    start=True,
                    stop=True,
                )

        def chunk(c):
            return slice(c * CHUNK, (c + 1) * CHUNK)

        stage_dealt(nc.scalar.copy, w2_staged, w2_raw[:], 1, 0)
        stage_dealt(nc.vector.tensor_copy, w2_staged, w2_raw[:], 0, 0)
        w2_mx = quantize(w2_staged, "w2")
        gather_noise(2)
        gather_noise(3)

        w1_staged = keep.tile([P, H * PACK], BF16, name="w1_staged", align_bytes=64)
        for u in range(2):
            stage_dealt(nc.scalar.copy, w1_staged[:], w1_raw[0][:], u, 0)

        w3_staged = keep.tile([P, N, PACK], BF16, name="w3_staged", align_bytes=64)
        inv_mag = []
        for c in range(CHUNKS):
            im = psum.tile([P, PACK, CHUNK], F32, name="im", tag="im")
            multiply(im, w2_mx, 0, (xw, xs), chunk(c))
            square = keep.tile([P, PACK, CHUNK], F32, name=f"square{c}")
            nc.scalar.activation(square[:], im[:], ACT.Square)
            last = c == CHUNKS - 1
            if last:
                nc.scalar.copy(
                    w3_staged[:].rearrange("p (c i) j -> p c j i", i=PAIR),
                    w3_raw[:].rearrange("p j (c i) -> p c j i", i=PAIR),
                )
            inv = keep.tile([P, PACK, CHUNK], F32, name=f"inv_mag{c}", tag="w3_raw" if last else f"inv_mag{c}")
            nc.scalar.activation(inv[:], square[:], ACT.Abs_reciprocal_sqrt, bias=quarter[:])
            inv_mag.append(inv)

        for u in range(2):
            stage_dealt(nc.vector.tensor_copy, w1_staged[:], w1_raw[1][:], u, P // 2)
        w1_mx = quantize(w1_staged[:], "w1")
        re = []
        for c in range(CHUNKS):
            bank = psum.tile([P, PACK, CHUNK], F32, name="re", tag="re")
            multiply(bank, w1_mx, 0, (xw, xs), chunk(c))
            re.append(bank)

        z_first = keep.tile([P, 2 * CHUNK, PACK], BF16, name="z_first", align_bytes=64)
        z_third = keep.tile([P, CHUNK, PACK], BF16, name="z_third", align_bytes=64)
        z_last = keep.tile([P, CHUNK, PACK], BF16, name="z_last", align_bytes=64)
        z = [z_first[:, chunk(0), :], z_first[:, chunk(1), :], z_third[:], z_last[:]]
        ratio = [keep.tile([P, PACK, CHUNK], F32, name=f"ratio{c}") for c in range(CHUNKS)]
        gain = [keep.tile([P, PACK, CHUNK], F32, name=f"gain{c}") for c in range(CHUNKS)]
        out_rows = out.rearrange("(a p) j -> p a j", p=P)

        def make_ratio(c):
            nc.vector.scalar_tensor_tensor(ratio[c][:], picked[:, :, chunk(c)], -1.0, inv_mag[c][:], ALU.mult, ALU.mult)

        def make_gain(c):
            nc.vector.tensor_scalar(gain[c][:], ratio[c][:], 1.0, 0.25, ALU.add, ALU.max)

        def make_z(c):
            nc.vector.tensor_tensor(
                z[c].rearrange("p (c i) t -> p c t i", i=PAIR),
                gain[c][:].rearrange("p t (c i) -> p c t i", i=PAIR),
                re[c][:].rearrange("p t (c i) -> p c t i", i=PAIR),
                ALU.mult,
            )

        def quantize_z(tile, name):
            return quantize(tile[:].rearrange("p n t -> p (n t)"), name)

        def emit(z_mx, frame0, first, count, tag, copy, queue):
            width = z_mx[0].shape[1]
            bank = psum.tile([P, count, width], F32, name="acc", tag=tag)
            multiply(bank, w3_mx, first, z_mx, slice(0, width))
            result = keep.tile([P, count, width], F32, name=f"result{frame0}_{first}")
            copy(result[:], bank[:])
            queue.dma_start(out_rows[:, first : first + count, frame0 : frame0 + width], result[:])

        make_ratio(0)
        make_ratio(1)
        make_gain(0)
        make_gain(1)
        make_z(0)
        make_z(1)
        make_ratio(2)
        z_first_mx = quantize_z(z_first, "z_first")
        make_gain(2)
        w3_mx = quantize(w3_staged[:].rearrange("p n j -> p (n j)"), "w3")
        for first in (0, 2):
            emit(z_first_mx, 0, first, 2, "im", nc.scalar.copy, nc.sync)
        make_ratio(3)
        make_z(2)
        make_gain(3)
        emit(quantize_z(z_third, "z_third"), 2 * CHUNK, 0, PACK, "im", nc.scalar.copy, nc.sync)
        make_z(3)
        z_last_mx = quantize_z(z_last, "z_last")
        emit(z_last_mx, 3 * CHUNK, 0, 2, "re", nc.scalar.copy, nc.scalar)
        emit(z_last_mx, 3 * CHUNK, 2, 2, "re", nc.vector.tensor_copy, nc.sync)
